import numpy as np
import ml_dtypes


def mxq(x, axis, fmt="e4m3"):
    dtype, down = {"e4m3": (ml_dtypes.float8_e4m3fn, 7), "e5m2": (ml_dtypes.float8_e5m2, 14)}[fmt]
    v = np.moveaxis(np.asarray(x, np.float32).astype(ml_dtypes.bfloat16).astype(np.float64), axis, -1)
    blocks = v.reshape(v.shape[:-1] + (-1, 32))
    amax = np.abs(blocks).max(-1, keepdims=True)
    byte = np.maximum(np.where(amax > 0, np.frexp(amax)[1] - 1 + 127, 0) - down, 1)
    scale = np.exp2(byte - 127.0)
    codes = (blocks / scale).astype(np.float32).astype(dtype).astype(np.float64)
    return np.moveaxis((codes * scale).reshape(v.shape), -1, axis)


WIDE = False


def mx_kscale(k):
    if not WIDE:
        return np.ones(k)
    levels = np.array([30, -30])
    if k % 512:
        return np.exp2(np.random.permutation(np.resize(levels, k // 32))).repeat(32)
    a = np.empty((k // 512, 16))
    for p in range(k // 512):
        a[p, :8] = np.random.permutation(np.resize(levels, 8))
        for g in range(8):
            far = levels[np.abs(levels - a[p, g]) >= 10]
            a[p, g + 8] = far[np.random.randint(len(far))]
    return np.exp2(a.ravel()).repeat(32)


def f64(x):
    return np.asarray(x).astype(np.float64)


def striped(idx):
    return np.tile(idx.reshape(-1, 16).T, (8, 1)).astype(np.uint16)


def unstriped(offs):
    return offs[:16].T.reshape(-1).astype(np.int64)


E2M1 = np.array([0.0, 0.5, 1.0, 1.5, 2.0, 3.0, 4.0, 6.0, -0.0, -0.5, -1.0, -1.5, -2.0, -3.0, -4.0, -6.0])


def pack_weight(w, fmt):
    k, n = w.shape
    w = f64(np.asarray(w, np.float32).astype(ml_dtypes.bfloat16)).reshape(k // 32, 32, n)
    amax = np.abs(w).max(1)
    if fmt == "e4m3":
        byte = np.frexp(amax)[1] - 1 + 127 - 7
    elif fmt == "e5m2":
        byte = np.frexp(amax)[1] - 1 + 127 - 14
    else:
        mant, ex = np.frexp(amax / 6.0)
        byte = np.where(mant > 0.5, ex, ex - 1) + 127
    byte = np.clip(np.where(amax > 0, byte, 1), 1, 254)
    scaled = (w * np.exp2(127.0 - byte)[:, None, :]).reshape(k, n).astype(np.float32)
    by_word = np.ascontiguousarray(scaled.reshape(k // 512, 128, 4, n).transpose(0, 1, 3, 2))
    if fmt == "e4m3":
        words = by_word.astype(ml_dtypes.float8_e4m3fn).view(np.uint8)
    elif fmt == "e5m2":
        words = by_word.astype(ml_dtypes.float8_e5m2).view(np.uint8)
    else:
        c = by_word.astype(ml_dtypes.float4_e2m1fn).view(np.uint8) & 0xF
        words = (c[..., 0::2] | (c[..., 1::2] << 4)).reshape(k // 512, 128, 2 * n)
    return np.ascontiguousarray(words), np.ascontiguousarray(byte.astype(np.uint8).reshape(k // 512, 16, n))


def unpack_weight(words, scales, fmt):
    g, _, n = scales.shape
    words = np.ascontiguousarray(words).reshape(g, 128, n, -1)
    if fmt == "e4m3":
        vals = words.view(ml_dtypes.float8_e4m3fn).astype(np.float64)
    elif fmt == "e5m2":
        vals = words.view(ml_dtypes.float8_e5m2).astype(np.float64)
    else:
        nib = np.empty((g, 128, n, 4), np.uint8)
        nib[..., 0::2] = words & 0xF
        nib[..., 1::2] = words >> 4
        vals = E2M1[nib]
    vals = vals * np.repeat(np.exp2(scales.astype(np.float64) - 127.0), 8, axis=1)[..., None]
    return vals.transpose(0, 1, 3, 2).reshape(g * 512, n)


def d_silu(v):
    s = 1.0 / (1.0 + np.exp(-np.maximum(v, -700.0)))
    return s * (1.0 + v * (1.0 - s))


K, T, E, C, H, N = 256, 1024, 4, 512, 512, 512


def by_expert(wq, xq):
    return np.concatenate([wq[e].T @ xq[:, e * C:(e + 1) * C] for e in range(E)], axis=1)


def setup_inputs():
    n = np.random.standard_normal
    v = mx_kscale(N)
    u = mx_kscale(H)
    first = np.random.permutation(np.repeat(np.arange(E), T // E))
    second = (first + 1 + np.random.permutation(np.repeat(np.arange(E - 1), -(-T // (E - 1)))[:T])) % E
    while np.bincount(second, minlength=E).max() != T // E:
        load = np.bincount(second, minlength=E); hi, lo = int(load.argmax()), int(load.argmin())
        t = np.flatnonzero((second == hi) & (first != lo))[0]; second[t] = lo
    slot_token = np.empty(E * C, np.int64); pos = np.empty((2, T), np.int64); fill = np.zeros(E, np.int64)
    place = np.stack([np.random.permutation(C) for _ in range(E)])
    for r, deal in enumerate((first, second)):
        for t in np.random.permutation(T):
            e = deal[t]; j = e * C + place[e, fill[e]]; fill[e] += 1; slot_token[j] = t; pos[r, t] = j
    g = np.random.uniform(0.2, 0.8, T)
    w_slot = np.empty(E * C); w_slot[pos[0]] = g; w_slot[pos[1]] = 1.0 - g
    dy = pack_weight(n((N, T)) * v[:, None], "e5m2")
    w2t = pack_weight(n((N, H)) / np.sqrt(N) / v[:, None] * u, "e4m3")
    w1t = [pack_weight(m, "e4m3") for m in n((E, H, K)) / np.sqrt(H) / u[None, :, None]]
    return {
        "dy_words": dy[0],
        "dy_scales": dy[1],
        "w2t_words": w2t[0],
        "w2t_scales": w2t[1],
        "w1t_words": np.stack([m[0] for m in w1t]),
        "w1t_scales": np.stack([m[1] for m in w1t]),
        "a": (n((H, E * C))).astype(np.float32),
        "gate": (np.tile(w_slot, (128, 1))).astype(np.float32),
        "offs": striped(slot_token),
        "pos1": striped(pos[0]),
        "pos2": striped(pos[1]),
    }


def reference(dy_words, dy_scales, w2t_words, w2t_scales, w1t_words, w1t_scales, a, gate, offs, pos1, pos2):
    w2t = unpack_weight(w2t_words, w2t_scales, "e4m3")
    w1t = np.stack([unpack_weight(w1t_words[e], w1t_scales[e], "e4m3") for e in range(E)])
    idx = unstriped(offs)
    dc = w2t.T @ unpack_weight(dy_words, dy_scales, "e5m2")
    da = f64(gate[:1]) * dc[:, idx] * d_silu(f64(a))
    dx = by_expert(w1t, mxq(da, 0, "e5m2"))
    out = dx[:, unstriped(pos1)] + dx[:, unstriped(pos2)]
    return out

@@ -1,0 +1,226 @@
+from contextlib import ExitStack
+
+import concourse.mybir as mybir
+from concourse.masks import make_identity
+
+K, T, E, C, H, N = 256, 1024, 4, 512, 512, 512
+S = E * C
+FLOPS = 2 * N * H * T + 2 * H * K * S
+
+F32 = mybir.dt.float32
+BF16 = mybir.dt.bfloat16
+I32 = mybir.dt.int32
+U16 = mybir.dt.uint16
+U8 = mybir.dt.uint8
+E4 = mybir.dt.float8_e4m3fn_x4
+E5 = mybir.dt.float8_e5m2_x4
+ALU = mybir.AluOpType
+ACT = mybir.ActivationFunctionType
+
+P = 128
+PACK = 4
+BANK = 512
+BLOCKS = S // P
+PER_E = C // P
+
+
+def tile_moe_sdb_silu_kernel(
+    tc, dy_words, dy_scales, w2t_words, w2t_scales, w1t_words, w1t_scales, a, gate, offs, pos1, pos2, out
+):
+    nc = tc.nc
+    with ExitStack() as ctx:
+        keep = ctx.enter_context(tc.tile_pool(name="keep", bufs=1))
+        work = ctx.enter_context(tc.tile_pool(name="work", bufs=2))
+        ring = ctx.enter_context(tc.psum_pool(name="ring", bufs=4))
+        fring = ctx.enter_context(tc.psum_pool(name="fring", bufs=4))
+
+        w2s_raw = keep.tile([P, H], U8, align_bytes=64)
+        dys = keep.tile([P, T], U8, align_bytes=64)
+        w1s = keep.tile([P, E, K], U8, align_bytes=64)
+        g_rows = keep.tile([P, P], F32)
+        ident = keep.tile([P, P], F32)
+        warm = keep.tile([P, 8], F32)
+        nc.vector.memset(w2s_raw[:].bitcast(I32), 0)
+        nc.vector.memset(dys[:].bitcast(I32), 0)
+        nc.vector.memset(warm[:, 0:1], 0.0)
+        nc.scalar.activation(warm[:, 4:5], warm[:, 0:1], ACT.Silu)
+        nc.gpsimd.memset(g_rows[:], 0.0)
+        make_identity(nc, ident[:])
+        nc.gpsimd.memset(w1s[:].bitcast(I32), 0)
+
+        w2_raw = keep.tile([P, H], I32)
+        nc.sync.dma_start(w2_raw[:], w2t_words[0].rearrange("p n d -> p (n d)").bitcast(I32))
+        dy_flat = dy_words[0].rearrange("p n d -> p (n d)")
+        dyw = [keep.tile([P, BANK], I32, name="dyw%d" % h, align_bytes=64) for h in range(2)]
+        nc.sync.dma_start(dyw[0][:], dy_flat[:, 0 : 4 * BANK].bitcast(I32))
+        for r in range(4):
+            nc.sync.dma_start(w2s_raw[r:P:32, :].bitcast(I32), w2t_scales[0, r:16:4, :].bitcast(I32))
+        for r in range(4):
+            nc.scalar.dma_start(dys[r:P:32, :].bitcast(I32), dy_scales[0, r:16:4, :].bitcast(I32))
+        nc.sync.dma_start(dyw[1][:], dy_flat[:, 4 * BANK : 8 * BANK].bitcast(I32))
+        offs_t = keep.tile([P, S // 16], U16)
+        nc.sync.dma_start(offs_t[:], offs)
+
+        a_rows = a.rearrange("(p t) j -> p t j", t=PACK)
+        a_of_block = {}
+
+        def load_a(j0, width):
+            piece = keep.tile([P, PACK, width], F32, name="a%d" % j0)
+            nc.sync.dma_start(piece[:], a_rows[:, :, j0 : j0 + width])
+            for o in range(0, width, P):
+                a_of_block[(j0 + o) // P] = (piece, o)
+
+        load_a(0, 256)
+        nc.sync.dma_start(g_rows[0:BLOCKS, :], gate[0, :].rearrange("(c x) -> c x", x=P))
+        load_a(256, 256)
+        load_a(512, 512)
+        w1w = keep.tile([P, E, K], I32, align_bytes=64)
+        nc.sync.dma_start(w1w[:], w1t_words[:, 0].rearrange("e p k d -> p e (k d)").bitcast(I32))
+        load_a(1024, 512)
+        for r in range(4):
+            nc.sync.dma_start(
+                w1s[r:P:32, :, :].bitcast(I32), w1t_scales[:, 0, r:16:4, :].rearrange("e q n -> q e n").bitcast(I32)
+            )
+        load_a(1536, 512)
+        pos1_t = keep.tile([P, T // 16], U16)
+        nc.sync.dma_start(pos1_t[:], pos1)
+        pos2_t = keep.tile([P, T // 16], U16)
+        nc.sync.dma_start(pos2_t[:], pos2)
+
+        w2w = keep.tile([P, H], I32, align_bytes=64)
+        w2s = keep.tile([P, H], U8, align_bytes=64)
+        nc.vector.tensor_copy(
+            w2w[:].rearrange("p (t m) -> p t m", t=PACK), w2_raw[:].rearrange("p (m t) -> p t m", t=PACK)
+        )
+        nc.vector.tensor_copy(
+            w2s[:].rearrange("p (t m) -> p m t", t=PACK), w2s_raw[:].rearrange("p (m t) -> p m t", t=PACK)
+        )
+
+        dc = [keep.tile([P, T], F32, name="dc%d" % t) for t in range(PACK)]
+        for t in range(PACK):
+            for h in range(2):
+                acc = ring.tile([P, BANK], F32, name="acc", tag="ring")
+                cols = slice(t * P, (t + 1) * P)
+                toks = slice(h * BANK, (h + 1) * BANK)
+                nc.tensor.matmul_mx(
+                    out=acc[:], lhsT=w2w[:, cols].bitcast(E4), lhsT_scale=w2s[:, cols],
+                    rhs=dyw[h][:].bitcast(E5), rhs_scale=dys[:, toks], start=True, stop=True,
+                )
+                if t == 0 and h == 1:
+                    nc.vector.tensor_copy(dc[t][:, toks], acc[:])
+                else:
+                    nc.scalar.copy(dc[t][:, toks], acc[:])
+
+        g_ps = ring.tile([P, BANK], F32, name="g_ps", tag="ring")
+        nc.tensor.transpose(g_ps[:, 0:P], g_rows[:], ident[:])
+        g_neg = keep.tile([P, BLOCKS], F32)
+        g_pos = keep.tile([P, BLOCKS], F32)
+        nc.scalar.activation(g_neg[:], g_ps[:, 0:BLOCKS], ACT.Copy, scale=-0.5)
+        nc.scalar.activation(g_pos[:], g_ps[:, 0:BLOCKS], ACT.Copy, scale=0.5)
+
+        dx = [keep.tile([P, S], F32, name="dx%d" % kt) for kt in range(K // P)]
+        gathered, th, z, y, da, daq, das = {}, {}, {}, {}, {}, {}, {}
+
+        def gather(e, ts):
+            if e not in gathered:
+                gathered[e] = work.tile([P, PACK, C], F32, name="gath", tag="gath", bufs=2)
+            for t in ts:
+                nc.vector.tensor_copy(gathered[e][:, t, :], dc[t][:].indirect(offs_t[:, e * C // 16 : (e + 1) * C // 16]))
+
+        def prep(b):
+            piece, o = a_of_block[b]
+            at = ring.tile([P, BANK], F32, name="at", tag="ring")
+            for t in range(PACK):
+                nc.tensor.transpose(at[:, t * P : (t + 1) * P], piece[:, t, o : o + P], ident[:])
+            pair, half = divmod(b, 2)
+            if half == 0:
+                th[pair] = work.tile([P, 2, BANK], F32, name="th", tag="th", bufs=3)
+                z[pair] = work.tile([P, 2, BANK], F32, name="z", tag="z", bufs=6)
+                y[pair] = work.tile([P, 2, BANK], F32, name="y", tag="y", bufs=6)
+            c = work.tile([P, BANK], F32, name="c", tag="c", bufs=4)
+            nc.scalar.activation(c[:], at[:], ACT.Silu, scale=-1.0)
+            nc.scalar.activation(th[pair][:, half, :], at[:], ACT.Tanh, scale=0.5)
+            if b % 3 == 0:
+                nc.gpsimd.tensor_scalar(z[pair][:, half, :], c[:], g_neg[:, b : b + 1], g_pos[:, b : b + 1], ALU.mult, ALU.add)
+            else:
+                nc.scalar.activation(z[pair][:, half, :], c[:], ACT.Identity, bias=g_pos[:, b : b + 1], scale=g_neg[:, b : b + 1])
+            if half == 1:
+                nc.gpsimd.tensor_tensor(y[pair][:], z[pair][:], th[pair][:], ALU.mult)
+
+        def finish(b):
+            e, blk = divmod(b, PER_E)
+            pair, half = divmod(b, 2)
+            f = fring.tile([P, BANK], F32, name="f", tag="f")
+            for t in range(PACK):
+                cols = slice(t * P, (t + 1) * P)
+                nc.tensor.matmul(f[:, cols], z[pair][:, half, cols], ident[:], start=True, stop=False, is_transpose=True)
+                nc.tensor.matmul(f[:, cols], y[pair][:, half, cols], ident[:], start=False, stop=True, is_transpose=True)
+            if blk == 0:
+                da[e] = work.tile([P, C * PACK], BF16, name="da", tag="da", bufs=2, align_bytes=64)
+            nc.vector.tensor_tensor(
+                da[e][:, blk * BANK : (blk + 1) * BANK].rearrange("p (c i t) -> p c t i", i=4, t=PACK),
+                gathered[e][:, :, blk * P : (blk + 1) * P].rearrange("p t (c i) -> p c t i", i=4),
+                f[:].rearrange("p (t c i) -> p c t i", t=PACK, i=4),
+                ALU.mult,
+            )
+
+        def quantize(e):
+            daq[e] = keep.tile([P, C], I32, name="daq%d" % e, align_bytes=64)
+            das[e] = keep.tile([P, C], U8, name="das%d" % e, align_bytes=64)
+            nc.vector.quantize_mx(out=daq[e][:].bitcast(E5), scales=das[e][:], in_=da[e][:])
+
+        def second(e):
+            for kt in range(K // P):
+                acc = ring.tile([P, BANK], F32, name="acc2", tag="ring")
+                cols = slice(kt * P, (kt + 1) * P)
+                nc.tensor.matmul_mx(
+                    out=acc[:], lhsT=w1w[:, e, cols].bitcast(E4), lhsT_scale=w1s[:, e, cols],
+                    rhs=daq[e][:].bitcast(E5), rhs_scale=das[e][:], start=True, stop=True,
+                )
+                if e == E - 1 and kt == 0:
+                    nc.vector.tensor_copy(dx[kt][:, e * C : (e + 1) * C], acc[:])
+                else:
+                    nc.scalar.copy(dx[kt][:, e * C : (e + 1) * C], acc[:])
+
+        gather(0, range(4))
+        for b in range(0, 4):
+            prep(b)
+        gather(1, range(4))
+        for b in range(4, 8):
+            prep(b)
+        for b in range(0, 4):
+            finish(b)
+        gather(2, [0])
+        quantize(0)
+        gather(2, [1, 2, 3])
+        prep(8)
+        second(0)
+        for b in range(9, 12):
+            prep(b)
+        for b in range(4, 8):
+            finish(b)
+        gather(3, [0])
+        quantize(1)
+        gather(3, [1, 2, 3])
+        prep(12)
+        prep(13)
+        second(1)
+        prep(14)
+        prep(15)
+        for b in range(8, 13):
+            finish(b)
+        quantize(2)
+        second(2)
+        for b in range(13, 16):
+            finish(b)
+        quantize(3)
+        second(3)
+
+        for kt, pieces in enumerate(([(0, 1024)], [(0, 512), (512, 256), (768, 256)])):
+            for t0, width in pieces:
+                first = keep.tile([P, width], F32, name="first%d_%d" % (kt, t0))
+                total = keep.tile([P, width], F32, name="total%d_%d" % (kt, t0))
+                lists = slice(t0 // 16, (t0 + width) // 16)
+                nc.vector.tensor_copy(first[:], dx[kt][:].indirect(pos1_t[:, lists]))
+                nc.vector.tensor_tensor(total[:], dx[kt][:].indirect(pos2_t[:, lists]), first[:], ALU.add)
+                nc.sync.dma_start(out[kt * P : (kt + 1) * P, t0 : t0 + width], total[:])

@@ -22,6 +22,8 @@ PACK = 4
 BANK = 512
 BLOCKS = S // P
 PER_E = C // P
+POOL_Z = (0, 2, 4, 6, 8)
+ZB = 4
 
 
 def tile_moe_sdb_silu_kernel(
@@ -40,26 +42,25 @@ def tile_moe_sdb_silu_kernel(
         g_rows = keep.tile([P, P], F32)
         ident = keep.tile([P, P], F32)
         warm = keep.tile([P, 8], F32)
-        nc.vector.memset(w2s_raw[:].bitcast(I32), 0)
-        nc.vector.memset(dys[:].bitcast(I32), 0)
-        nc.vector.memset(warm[:, 0:1], 0.0)
-        nc.scalar.activation(warm[:, 4:5], warm[:, 0:1], ACT.Silu)
+        nc.gpsimd.memset(dys[:].bitcast(I32), 0)
+        nc.gpsimd.memset(w2s_raw[:].bitcast(I32), 0)
+        nc.gpsimd.memset(warm[:, 0:1], 0.0)
         nc.gpsimd.memset(g_rows[:], 0.0)
         make_identity(nc, ident[:])
         nc.gpsimd.memset(w1s[:].bitcast(I32), 0)
 
-        w2_raw = keep.tile([P, H], I32)
-        nc.sync.dma_start(w2_raw[:], w2t_words[0].rearrange("p n d -> p (n d)").bitcast(I32))
-        dy_flat = dy_words[0].rearrange("p n d -> p (n d)")
-        dyw = [keep.tile([P, BANK], I32, name="dyw%d" % h, align_bytes=64) for h in range(2)]
-        nc.sync.dma_start(dyw[0][:], dy_flat[:, 0 : 4 * BANK].bitcast(I32))
-        for r in range(4):
-            nc.sync.dma_start(w2s_raw[r:P:32, :].bitcast(I32), w2t_scales[0, r:16:4, :].bitcast(I32))
-        for r in range(4):
-            nc.scalar.dma_start(dys[r:P:32, :].bitcast(I32), dy_scales[0, r:16:4, :].bitcast(I32))
-        nc.sync.dma_start(dyw[1][:], dy_flat[:, 4 * BANK : 8 * BANK].bitcast(I32))
         offs_t = keep.tile([P, S // 16], U16)
         nc.sync.dma_start(offs_t[:], offs)
+        for r in range(4):
+            nc.scalar.dma_start(w2s_raw[r:P:32, :].bitcast(I32), w2t_scales[0, r:16:4, :].bitcast(I32))
+        nc.scalar.activation(warm[:, 4:5], warm[:, 0:1], ACT.Silu)
+        w2_raw = keep.tile([P, H], I32)
+        dyw = keep.tile([P, T], I32, align_bytes=64)
+        for r in range(4):
+            nc.sync.dma_start(dys[r:P:32, :].bitcast(I32), dy_scales[0, r:16:4, :].bitcast(I32))
+            if r == 0:
+                nc.sync.dma_start(w2_raw[:], w2t_words[0].rearrange("p n d -> p (n d)").bitcast(I32))
+                nc.sync.dma_start(dyw[:], dy_words[0].rearrange("p n d -> p (n d)").bitcast(I32))
 
         a_rows = a.rearrange("(p t) j -> p t j", t=PACK)
         a_of_block = {}
@@ -70,6 +71,10 @@ def tile_moe_sdb_silu_kernel(
             for o in range(0, width, P):
                 a_of_block[(j0 + o) // P] = (piece, o)
 
+        gate_last = []
+        for h, tag in enumerate(("even", "odd")):
+            gate_last.append(keep.tile([P, C // 2], F32, name="gate_last%d" % h, tag=tag))
+            nc.sync.dma_start(gate_last[h][:], gate[:, (E - 1) * C + h * C // 2 : (E - 1) * C + (h + 1) * C // 2])
         load_a(0, 256)
         nc.sync.dma_start(g_rows[0:BLOCKS, :], gate[0, :].rearrange("(c x) -> c x", x=P))
         load_a(256, 256)
@@ -97,34 +102,43 @@ def tile_moe_sdb_silu_kernel(
         )
 
         dc = [keep.tile([P, T], F32, name="dc%d" % t) for t in range(PACK)]
-        for t in range(PACK):
+        dx = [keep.tile([P, S], F32, name="dx%d" % kt) for kt in range(K // P)]
+        g_neg = keep.tile([P, BLOCKS], F32)
+        g_pos = keep.tile([P, BLOCKS], F32)
+        da = keep.tile([P, S * PACK], BF16, align_bytes=64)
+        daq = keep.tile([P, S], I32, align_bytes=64)
+        das = keep.tile([P, S], U8, align_bytes=64)
+        gathered, th, z, y = {}, {}, {}, {}
+
+        def first_product(t):
             for h in range(2):
                 acc = ring.tile([P, BANK], F32, name="acc", tag="ring")
                 cols = slice(t * P, (t + 1) * P)
                 toks = slice(h * BANK, (h + 1) * BANK)
                 nc.tensor.matmul_mx(
                     out=acc[:], lhsT=w2w[:, cols].bitcast(E4), lhsT_scale=w2s[:, cols],
-                    rhs=dyw[h][:].bitcast(E5), rhs_scale=dys[:, toks], start=True, stop=True,
+                    rhs=dyw[:, toks].bitcast(E5), rhs_scale=dys[:, toks], start=True, stop=True,
                 )
                 if t == 0 and h == 1:
                     nc.vector.tensor_copy(dc[t][:, toks], acc[:])
                 else:
                     nc.scalar.copy(dc[t][:, toks], acc[:])
 
-        g_ps = ring.tile([P, BANK], F32, name="g_ps", tag="ring")
-        nc.tensor.transpose(g_ps[:, 0:P], g_rows[:], ident[:])
-        g_neg = keep.tile([P, BLOCKS], F32)
-        g_pos = keep.tile([P, BLOCKS], F32)
-        nc.scalar.activation(g_neg[:], g_ps[:, 0:BLOCKS], ACT.Copy, scale=-0.5)
-        nc.scalar.activation(g_pos[:], g_ps[:, 0:BLOCKS], ACT.Copy, scale=0.5)
+        def gates_to_partitions():
+            g_ps = ring.tile([P, BANK], F32, name="g_ps", tag="ring")
+            nc.tensor.transpose(g_ps[:, 0:P], g_rows[:], ident[:])
+            nc.scalar.activation(g_neg[:], g_ps[:, 0:BLOCKS], ACT.Copy, scale=-0.5)
+            nc.scalar.activation(g_pos[:], g_ps[:, 0:BLOCKS], ACT.Copy, scale=0.5)
 
-        dx = [keep.tile([P, S], F32, name="dx%d" % kt) for kt in range(K // P)]
-        gathered, th, z, y, da, daq, das = {}, {}, {}, {}, {}, {}, {}
-
-        def gather(e, ts):
+        def gather(e, t):
             if e not in gathered:
-                gathered[e] = work.tile([P, PACK, C], F32, name="gath", tag="gath", bufs=2)
-            for t in ts:
+                gathered[e] = keep.tile([P, PACK, C], F32, name="gath%d" % e, tag=("even", "odd", "even", "last")[e])
+            if e == E - 1:
+                for h in range(2):
+                    j0 = e * C + h * C // 2
+                    window = dc[t][:].indirect(offs_t[:, j0 // 16 : (j0 + C // 2) // 16])
+                    nc.vector.tensor_tensor(gathered[e][:, t, h * C // 2 : (h + 1) * C // 2], window, gate_last[h][:], ALU.mult)
+            else:
                 nc.vector.tensor_copy(gathered[e][:, t, :], dc[t][:].indirect(offs_t[:, e * C // 16 : (e + 1) * C // 16]))
 
         def prep(b):
@@ -135,17 +149,20 @@ def tile_moe_sdb_silu_kernel(
             pair, half = divmod(b, 2)
             if half == 0:
                 th[pair] = work.tile([P, 2, BANK], F32, name="th", tag="th", bufs=3)
-                z[pair] = work.tile([P, 2, BANK], F32, name="z", tag="z", bufs=6)
-                y[pair] = work.tile([P, 2, BANK], F32, name="y", tag="y", bufs=6)
+                z[pair] = work.tile([P, 2, BANK], F32, name="z", tag="z", bufs=ZB)
+                y[pair] = work.tile([P, 2, BANK], F32, name="y", tag="y", bufs=ZB)
             c = work.tile([P, BANK], F32, name="c", tag="c", bufs=4)
             nc.scalar.activation(c[:], at[:], ACT.Silu, scale=-1.0)
             nc.scalar.activation(th[pair][:, half, :], at[:], ACT.Tanh, scale=0.5)
-            if b % 3 == 0:
+            if b in POOL_Z:
                 nc.gpsimd.tensor_scalar(z[pair][:, half, :], c[:], g_neg[:, b : b + 1], g_pos[:, b : b + 1], ALU.mult, ALU.add)
             else:
                 nc.scalar.activation(z[pair][:, half, :], c[:], ACT.Identity, bias=g_pos[:, b : b + 1], scale=g_neg[:, b : b + 1])
             if half == 1:
                 nc.gpsimd.tensor_tensor(y[pair][:], z[pair][:], th[pair][:], ALU.mult)
+
+        def da_view(j0, width):
+            return da[:, j0 * PACK : (j0 + width) * PACK].rearrange("p (c i t) -> p c t i", i=4, t=PACK)
 
         def finish(b):
             e, blk = divmod(b, PER_E)
@@ -153,67 +170,95 @@ def tile_moe_sdb_silu_kernel(
             f = fring.tile([P, BANK], F32, name="f", tag="f")
             for t in range(PACK):
                 cols = slice(t * P, (t + 1) * P)
-                nc.tensor.matmul(f[:, cols], z[pair][:, half, cols], ident[:], start=True, stop=False, is_transpose=True)
-                nc.tensor.matmul(f[:, cols], y[pair][:, half, cols], ident[:], start=False, stop=True, is_transpose=True)
-            if blk == 0:
-                da[e] = work.tile([P, C * PACK], BF16, name="da", tag="da", bufs=2, align_bytes=64)
+                nc.tensor.matmul(f[:, cols], y[pair][:, half, cols], ident[:], start=True, stop=False, is_transpose=True)
+                nc.tensor.matmul(f[:, cols], z[pair][:, half, cols], ident[:], start=False, stop=True, is_transpose=True)
             nc.vector.tensor_tensor(
-                da[e][:, blk * BANK : (blk + 1) * BANK].rearrange("p (c i t) -> p c t i", i=4, t=PACK),
+                da_view(b * P, P),
                 gathered[e][:, :, blk * P : (blk + 1) * P].rearrange("p t (c i) -> p c t i", i=4),
                 f[:].rearrange("p (t c i) -> p c t i", t=PACK, i=4),
                 ALU.mult,
             )
 
-        def quantize(e):
-            daq[e] = keep.tile([P, C], I32, name="daq%d" % e, align_bytes=64)
-            das[e] = keep.tile([P, C], U8, name="das%d" % e, align_bytes=64)
-            nc.vector.quantize_mx(out=daq[e][:].bitcast(E5), scales=das[e][:], in_=da[e][:])
+        HALF = C // 2
+        plain = {}
+
+        def prep_plain(h):
+            piece, o = a_of_block[(E - 1) * PER_E]
+            v = piece[:, :, h * HALF : (h + 1) * HALF]
+            cp = work.tile([P, PACK, HALF], F32, name="cp", tag="cp")
+            tp = work.tile([P, PACK, HALF], F32, name="tp", tag="tp")
+            zp = work.tile([P, PACK, HALF], F32, name="zp", tag="zp")
+            nc.scalar.activation(cp[:], v, ACT.Silu, scale=-1.0)
+            nc.scalar.activation(tp[:], v, ACT.Tanh, scale=0.5)
+            nc.scalar.activation(zp[:], cp[:], ACT.Copy, bias=0.5, scale=-0.5)
+            plain[h] = (tp, zp)
+
+        def derive_plain(h):
+            tp, zp = plain[h]
+            dp = work.tile([P, PACK, HALF], F32, name="dp", tag="dp")
+            nc.vector.scalar_tensor_tensor(dp[:], tp[:], 1.0, zp[:], ALU.add, ALU.mult)
+            plain[h] = dp
+
+        def finish_plain(h):
+            nc.vector.tensor_tensor(
+                da_view((E - 1) * C + h * HALF, HALF),
+                gathered[E - 1][:, :, h * HALF : (h + 1) * HALF].rearrange("p t (c i) -> p c t i", i=4),
+                plain[h][:].rearrange("p t (c i) -> p c t i", i=4),
+                ALU.mult,
+            )
+
+        def quantize(j0, width):
+            nc.vector.quantize_mx(
+                out=daq[:, j0 : j0 + width].bitcast(E5), scales=das[:, j0 : j0 + width],
+                in_=da[:, j0 * PACK : (j0 + width) * PACK],
+            )
 
         def second(e):
+            slots = slice(e * C, (e + 1) * C)
             for kt in range(K // P):
                 acc = ring.tile([P, BANK], F32, name="acc2", tag="ring")
                 cols = slice(kt * P, (kt + 1) * P)
                 nc.tensor.matmul_mx(
                     out=acc[:], lhsT=w1w[:, e, cols].bitcast(E4), lhsT_scale=w1s[:, e, cols],
-                    rhs=daq[e][:].bitcast(E5), rhs_scale=das[e][:], start=True, stop=True,
+                    rhs=daq[:, slots].bitcast(E5), rhs_scale=das[:, slots], start=True, stop=True,
                 )
                 if e == E - 1 and kt == 0:
-                    nc.vector.tensor_copy(dx[kt][:, e * C : (e + 1) * C], acc[:])
+                    nc.vector.tensor_copy(dx[kt][:, slots], acc[:])
                 else:
-                    nc.scalar.copy(dx[kt][:, e * C : (e + 1) * C], acc[:])
+                    nc.scalar.copy(dx[kt][:, slots], acc[:])
 
-        gather(0, range(4))
-        for b in range(0, 4):
-            prep(b)
-        gather(1, range(4))
-        for b in range(4, 8):
+        first_product(0)
+        gather(3, 0)
+        for t in range(1, PACK):
+            first_product(t)
+            gather(3, t)
+        gates_to_partitions()
+        for e in range(2):
+            for t in range(PACK):
+                gather(e, t)
+        for b in range(0, 8):
             prep(b)
         for b in range(0, 4):
             finish(b)
-        gather(2, [0])
-        quantize(0)
-        gather(2, [1, 2, 3])
-        prep(8)
+        for t in range(PACK):
+            gather(2, t)
+        for b in range(8, 12):
+            prep(b)
+        for b in range(4, 12):
+            finish(b)
+        prep_plain(0)
+        prep_plain(1)
+        quantize(0, 2 * C)
         second(0)
-        for b in range(9, 12):
-            prep(b)
-        for b in range(4, 8):
-            finish(b)
-        gather(3, [0])
-        quantize(1)
-        gather(3, [1, 2, 3])
-        prep(12)
-        prep(13)
         second(1)
-        prep(14)
-        prep(15)
-        for b in range(8, 13):
-            finish(b)
-        quantize(2)
+        derive_plain(0)
+        quantize(2 * C, C)
         second(2)
-        for b in range(13, 16):
-            finish(b)
-        quantize(3)
+        finish_plain(0)
+        derive_plain(1)
+        quantize(3 * C, HALF)
+        finish_plain(1)
+        quantize(3 * C + HALF, HALF)
         second(3)
 
         for kt, pieces in enumerate(([(0, 1024)], [(0, 512), (512, 256), (768, 256)])):

from contextlib import ExitStack

import concourse.mybir as mybir
from concourse.masks import make_identity

K, T, E, C, H, N = 256, 1024, 4, 512, 512, 512
S = E * C
FLOPS = 2 * N * H * T + 2 * H * K * S

F32 = mybir.dt.float32
BF16 = mybir.dt.bfloat16
I32 = mybir.dt.int32
U16 = mybir.dt.uint16
U8 = mybir.dt.uint8
E4 = mybir.dt.float8_e4m3fn_x4
E5 = mybir.dt.float8_e5m2_x4
ALU = mybir.AluOpType
ACT = mybir.ActivationFunctionType

P = 128
PACK = 4
BANK = 512
BLOCKS = S // P
PER_E = C // P
POOL_Z = (0, 2, 4, 6, 8)
ZB = 4


def tile_moe_sdb_silu_kernel(
    tc, dy_words, dy_scales, w2t_words, w2t_scales, w1t_words, w1t_scales, a, gate, offs, pos1, pos2, out
):
    nc = tc.nc
    with ExitStack() as ctx:
        keep = ctx.enter_context(tc.tile_pool(name="keep", bufs=1))
        work = ctx.enter_context(tc.tile_pool(name="work", bufs=2))
        ring = ctx.enter_context(tc.psum_pool(name="ring", bufs=4))
        fring = ctx.enter_context(tc.psum_pool(name="fring", bufs=4))

        w2s_raw = keep.tile([P, H], U8, align_bytes=64)
        dys = keep.tile([P, T], U8, align_bytes=64)
        w1s = keep.tile([P, E, K], U8, align_bytes=64)
        g_rows = keep.tile([P, P], F32)
        ident = keep.tile([P, P], F32)
        warm = keep.tile([P, 8], F32)
        nc.gpsimd.memset(dys[:].bitcast(I32), 0)
        nc.gpsimd.memset(w2s_raw[:].bitcast(I32), 0)
        nc.gpsimd.memset(warm[:, 0:1], 0.0)
        nc.gpsimd.memset(g_rows[:], 0.0)
        make_identity(nc, ident[:])
        nc.gpsimd.memset(w1s[:].bitcast(I32), 0)

        offs_t = keep.tile([P, S // 16], U16)
        nc.sync.dma_start(offs_t[:], offs)
        for r in range(4):
            nc.scalar.dma_start(w2s_raw[r:P:32, :].bitcast(I32), w2t_scales[0, r:16:4, :].bitcast(I32))
        nc.scalar.activation(warm[:, 4:5], warm[:, 0:1], ACT.Silu)
        w2_raw = keep.tile([P, H], I32)
        dyw = keep.tile([P, T], I32, align_bytes=64)
        for r in range(4):
            nc.sync.dma_start(dys[r:P:32, :].bitcast(I32), dy_scales[0, r:16:4, :].bitcast(I32))
            if r == 0:
                nc.sync.dma_start(w2_raw[:], w2t_words[0].rearrange("p n d -> p (n d)").bitcast(I32))
                nc.sync.dma_start(dyw[:], dy_words[0].rearrange("p n d -> p (n d)").bitcast(I32))

        a_rows = a.rearrange("(p t) j -> p t j", t=PACK)
        a_of_block = {}

        def load_a(j0, width):
            piece = keep.tile([P, PACK, width], F32, name="a%d" % j0)
            nc.sync.dma_start(piece[:], a_rows[:, :, j0 : j0 + width])
            for o in range(0, width, P):
                a_of_block[(j0 + o) // P] = (piece, o)

        gate_last = []
        for h, tag in enumerate(("even", "odd")):
            gate_last.append(keep.tile([P, C // 2], F32, name="gate_last%d" % h, tag=tag))
            nc.sync.dma_start(gate_last[h][:], gate[:, (E - 1) * C + h * C // 2 : (E - 1) * C + (h + 1) * C // 2])
        load_a(0, 256)
        nc.sync.dma_start(g_rows[0:BLOCKS, :], gate[0, :].rearrange("(c x) -> c x", x=P))
        load_a(256, 256)
        load_a(512, 512)
        w1w = keep.tile([P, E, K], I32, align_bytes=64)
        nc.sync.dma_start(w1w[:], w1t_words[:, 0].rearrange("e p k d -> p e (k d)").bitcast(I32))
        load_a(1024, 512)
        for r in range(4):
            nc.sync.dma_start(
                w1s[r:P:32, :, :].bitcast(I32), w1t_scales[:, 0, r:16:4, :].rearrange("e q n -> q e n").bitcast(I32)
            )
        load_a(1536, 512)
        pos1_t = keep.tile([P, T // 16], U16)
        nc.sync.dma_start(pos1_t[:], pos1)
        pos2_t = keep.tile([P, T // 16], U16)
        nc.sync.dma_start(pos2_t[:], pos2)

        w2w = keep.tile([P, H], I32, align_bytes=64)
        w2s = keep.tile([P, H], U8, align_bytes=64)
        nc.vector.tensor_copy(
            w2w[:].rearrange("p (t m) -> p t m", t=PACK), w2_raw[:].rearrange("p (m t) -> p t m", t=PACK)
        )
        nc.vector.tensor_copy(
            w2s[:].rearrange("p (t m) -> p m t", t=PACK), w2s_raw[:].rearrange("p (m t) -> p m t", t=PACK)
        )

        dc = [keep.tile([P, T], F32, name="dc%d" % t) for t in range(PACK)]
        dx = [keep.tile([P, S], F32, name="dx%d" % kt) for kt in range(K // P)]
        g_neg = keep.tile([P, BLOCKS], F32)
        g_pos = keep.tile([P, BLOCKS], F32)
        da = keep.tile([P, S * PACK], BF16, align_bytes=64)
        daq = keep.tile([P, S], I32, align_bytes=64)
        das = keep.tile([P, S], U8, align_bytes=64)
        gathered, th, z, y = {}, {}, {}, {}

        def first_product(t):
            for h in range(2):
                acc = ring.tile([P, BANK], F32, name="acc", tag="ring")
                cols = slice(t * P, (t + 1) * P)
                toks = slice(h * BANK, (h + 1) * BANK)
                nc.tensor.matmul_mx(
                    out=acc[:], lhsT=w2w[:, cols].bitcast(E4), lhsT_scale=w2s[:, cols],
                    rhs=dyw[:, toks].bitcast(E5), rhs_scale=dys[:, toks], start=True, stop=True,
                )
                if t == 0 and h == 1:
                    nc.vector.tensor_copy(dc[t][:, toks], acc[:])
                else:
                    nc.scalar.copy(dc[t][:, toks], acc[:])

        def gates_to_partitions():
            g_ps = ring.tile([P, BANK], F32, name="g_ps", tag="ring")
            nc.tensor.transpose(g_ps[:, 0:P], g_rows[:], ident[:])
            nc.scalar.activation(g_neg[:], g_ps[:, 0:BLOCKS], ACT.Copy, scale=-0.5)
            nc.scalar.activation(g_pos[:], g_ps[:, 0:BLOCKS], ACT.Copy, scale=0.5)

        def gather(e, t):
            if e not in gathered:
                gathered[e] = keep.tile([P, PACK, C], F32, name="gath%d" % e, tag=("even", "odd", "even", "last")[e])
            if e == E - 1:
                for h in range(2):
                    j0 = e * C + h * C // 2
                    window = dc[t][:].indirect(offs_t[:, j0 // 16 : (j0 + C // 2) // 16])
                    nc.vector.tensor_tensor(gathered[e][:, t, h * C // 2 : (h + 1) * C // 2], window, gate_last[h][:], ALU.mult)
            else:
                nc.vector.tensor_copy(gathered[e][:, t, :], dc[t][:].indirect(offs_t[:, e * C // 16 : (e + 1) * C // 16]))

        def prep(b):
            piece, o = a_of_block[b]
            at = ring.tile([P, BANK], F32, name="at", tag="ring")
            for t in range(PACK):
                nc.tensor.transpose(at[:, t * P : (t + 1) * P], piece[:, t, o : o + P], ident[:])
            pair, half = divmod(b, 2)
            if half == 0:
                th[pair] = work.tile([P, 2, BANK], F32, name="th", tag="th", bufs=3)
                z[pair] = work.tile([P, 2, BANK], F32, name="z", tag="z", bufs=ZB)
                y[pair] = work.tile([P, 2, BANK], F32, name="y", tag="y", bufs=ZB)
            c = work.tile([P, BANK], F32, name="c", tag="c", bufs=4)
            nc.scalar.activation(c[:], at[:], ACT.Silu, scale=-1.0)
            nc.scalar.activation(th[pair][:, half, :], at[:], ACT.Tanh, scale=0.5)
            if b in POOL_Z:
                nc.gpsimd.tensor_scalar(z[pair][:, half, :], c[:], g_neg[:, b : b + 1], g_pos[:, b : b + 1], ALU.mult, ALU.add)
            else:
                nc.scalar.activation(z[pair][:, half, :], c[:], ACT.Identity, bias=g_pos[:, b : b + 1], scale=g_neg[:, b : b + 1])
            if half == 1:
                nc.gpsimd.tensor_tensor(y[pair][:], z[pair][:], th[pair][:], ALU.mult)

        def da_view(j0, width):
            return da[:, j0 * PACK : (j0 + width) * PACK].rearrange("p (c i t) -> p c t i", i=4, t=PACK)

        def finish(b):
            e, blk = divmod(b, PER_E)
            pair, half = divmod(b, 2)
            f = fring.tile([P, BANK], F32, name="f", tag="f")
            for t in range(PACK):
                cols = slice(t * P, (t + 1) * P)
                nc.tensor.matmul(f[:, cols], y[pair][:, half, cols], ident[:], start=True, stop=False, is_transpose=True)
                nc.tensor.matmul(f[:, cols], z[pair][:, half, cols], ident[:], start=False, stop=True, is_transpose=True)
            nc.vector.tensor_tensor(
                da_view(b * P, P),
                gathered[e][:, :, blk * P : (blk + 1) * P].rearrange("p t (c i) -> p c t i", i=4),
                f[:].rearrange("p (t c i) -> p c t i", t=PACK, i=4),
                ALU.mult,
            )

        HALF = C // 2
        plain = {}

        def prep_plain(h):
            piece, o = a_of_block[(E - 1) * PER_E]
            v = piece[:, :, h * HALF : (h + 1) * HALF]
            cp = work.tile([P, PACK, HALF], F32, name="cp", tag="cp")
            tp = work.tile([P, PACK, HALF], F32, name="tp", tag="tp")
            zp = work.tile([P, PACK, HALF], F32, name="zp", tag="zp")
            nc.scalar.activation(cp[:], v, ACT.Silu, scale=-1.0)
            nc.scalar.activation(tp[:], v, ACT.Tanh, scale=0.5)
            nc.scalar.activation(zp[:], cp[:], ACT.Copy, bias=0.5, scale=-0.5)
            plain[h] = (tp, zp)

        def derive_plain(h):
            tp, zp = plain[h]
            dp = work.tile([P, PACK, HALF], F32, name="dp", tag="dp")
            nc.vector.scalar_tensor_tensor(dp[:], tp[:], 1.0, zp[:], ALU.add, ALU.mult)
            plain[h] = dp

        def finish_plain(h):
            nc.vector.tensor_tensor(
                da_view((E - 1) * C + h * HALF, HALF),
                gathered[E - 1][:, :, h * HALF : (h + 1) * HALF].rearrange("p t (c i) -> p c t i", i=4),
                plain[h][:].rearrange("p t (c i) -> p c t i", i=4),
                ALU.mult,
            )

        def quantize(j0, width):
            nc.vector.quantize_mx(
                out=daq[:, j0 : j0 + width].bitcast(E5), scales=das[:, j0 : j0 + width],
                in_=da[:, j0 * PACK : (j0 + width) * PACK],
            )

        def second(e):
            slots = slice(e * C, (e + 1) * C)
            for kt in range(K // P):
                acc = ring.tile([P, BANK], F32, name="acc2", tag="ring")
                cols = slice(kt * P, (kt + 1) * P)
                nc.tensor.matmul_mx(
                    out=acc[:], lhsT=w1w[:, e, cols].bitcast(E4), lhsT_scale=w1s[:, e, cols],
                    rhs=daq[:, slots].bitcast(E5), rhs_scale=das[:, slots], start=True, stop=True,
                )
                if e == E - 1 and kt == 0:
                    nc.vector.tensor_copy(dx[kt][:, slots], acc[:])
                else:
                    nc.scalar.copy(dx[kt][:, slots], acc[:])

        first_product(0)
        gather(3, 0)
        for t in range(1, PACK):
            first_product(t)
            gather(3, t)
        gates_to_partitions()
        for e in range(2):
            for t in range(PACK):
                gather(e, t)
        for b in range(0, 8):
            prep(b)
        for b in range(0, 4):
            finish(b)
        for t in range(PACK):
            gather(2, t)
        for b in range(8, 12):
            prep(b)
        for b in range(4, 12):
            finish(b)
        prep_plain(0)
        prep_plain(1)
        quantize(0, 2 * C)
        second(0)
        second(1)
        derive_plain(0)
        quantize(2 * C, C)
        second(2)
        finish_plain(0)
        derive_plain(1)
        quantize(3 * C, HALF)
        finish_plain(1)
        quantize(3 * C + HALF, HALF)
        second(3)

        for kt, pieces in enumerate(([(0, 1024)], [(0, 512), (512, 256), (768, 256)])):
            for t0, width in pieces:
                first = keep.tile([P, width], F32, name="first%d_%d" % (kt, t0))
                total = keep.tile([P, width], F32, name="total%d_%d" % (kt, t0))
                lists = slice(t0 // 16, (t0 + width) // 16)
                nc.vector.tensor_copy(first[:], dx[kt][:].indirect(pos1_t[:, lists]))
                nc.vector.tensor_tensor(total[:], dx[kt][:].indirect(pos2_t[:, lists]), first[:], ALU.add)
                nc.sync.dma_start(out[kt * P : (kt + 1) * P, t0 : t0 + width], total[:])
